import numpy as np
import ml_dtypes


def mxq(x, axis, fmt="e4m3"):
    dtype, down = {"e4m3": (ml_dtypes.float8_e4m3fn, 7), "e5m2": (ml_dtypes.float8_e5m2, 14)}[fmt]
    v = np.moveaxis(np.asarray(x, np.float32).astype(ml_dtypes.bfloat16).astype(np.float64), axis, -1)
    blocks = v.reshape(v.shape[:-1] + (-1, 32))
    amax = np.abs(blocks).max(-1, keepdims=True)
    byte = np.maximum(np.where(amax > 0, np.frexp(amax)[1] - 1 + 127, 0) - down, 1)
    scale = np.exp2(byte - 127.0)
    codes = (blocks / scale).astype(np.float32).astype(dtype).astype(np.float64)
    return np.moveaxis((codes * scale).reshape(v.shape), -1, axis)


WIDE = False


def mx_kscale(k):
    if not WIDE:
        return np.ones(k)
    levels = np.array([10, -10, 5, -5, 0])
    if k % 512:
        return np.exp2(np.random.permutation(np.resize(levels, k // 32))).repeat(32)
    a = np.empty((k // 512, 16))
    for p in range(k // 512):
        a[p, :8] = np.random.permutation(np.resize(levels, 8))
        for g in range(8):
            far = levels[np.abs(levels - a[p, g]) >= 10]
            a[p, g + 8] = far[np.random.randint(len(far))]
    return np.exp2(a.ravel()).repeat(32)


def f64(x):
    return np.asarray(x).astype(np.float64)


def striped(idx):
    return np.tile(idx.reshape(-1, 16).T, (8, 1)).astype(np.uint16)


def unstriped(offs):
    return offs[:16].T.reshape(-1).astype(np.int64)


E2M1 = np.array([0.0, 0.5, 1.0, 1.5, 2.0, 3.0, 4.0, 6.0, -0.0, -0.5, -1.0, -1.5, -2.0, -3.0, -4.0, -6.0])


def pack_weight(w, fmt):
    k, n = w.shape
    w = f64(np.asarray(w, np.float32).astype(ml_dtypes.bfloat16)).reshape(k // 32, 32, n)
    amax = np.abs(w).max(1)
    if fmt == "e4m3":
        byte = np.frexp(amax)[1] - 1 + 127 - 7
    else:
        mant, ex = np.frexp(amax / 6.0)
        byte = np.where(mant > 0.5, ex, ex - 1) + 127
    byte = np.clip(np.where(amax > 0, byte, 1), 1, 254)
    scaled = (w * np.exp2(127.0 - byte)[:, None, :]).reshape(k, n).astype(np.float32)
    by_word = np.ascontiguousarray(scaled.reshape(k // 512, 128, 4, n).transpose(0, 1, 3, 2))
    if fmt == "e4m3":
        words = by_word.astype(ml_dtypes.float8_e4m3fn).view(np.uint8)
    else:
        c = by_word.astype(ml_dtypes.float4_e2m1fn).view(np.uint8) & 0xF
        words = (c[..., 0::2] | (c[..., 1::2] << 4)).reshape(k // 512, 128, 2 * n)
    return np.ascontiguousarray(words), np.ascontiguousarray(byte.astype(np.uint8).reshape(k // 512, 16, n))


def unpack_weight(words, scales, fmt):
    g, _, n = scales.shape
    words = np.ascontiguousarray(words).reshape(g, 128, n, -1)
    if fmt == "e4m3":
        vals = words.view(ml_dtypes.float8_e4m3fn).astype(np.float64)
    else:
        nib = np.empty((g, 128, n, 4), np.uint8)
        nib[..., 0::2] = words & 0xF
        nib[..., 1::2] = words >> 4
        vals = E2M1[nib]
    vals = vals * np.repeat(np.exp2(scales.astype(np.float64) - 127.0), 8, axis=1)[..., None]
    return vals.transpose(0, 1, 3, 2).reshape(g * 512, n)


K, T, E, C, N = 2560, 640, 2, 256, 512
M = 256


def by_expert(wq, xq):
    return np.concatenate([wq[e].T @ xq[:, e * C:(e + 1) * C] for e in range(E)], axis=1)


def setup_inputs():
    n = np.random.standard_normal
    s = mx_kscale(K)[:, None]
    v = mx_kscale(N)
    w = [pack_weight(m, "e2m1") for m in n((E, K, N)) / np.sqrt(K) / s[None] * v[None, None, :]]
    return {
        "xT": (n((K, T)) * s).astype(np.float32),
        "w_words": np.stack([m[0] for m in w]),
        "w_scales": np.stack([m[1] for m in w]),
        "b": (0.3 * n((N, E)) * v[:, None]).astype(np.float32),
        "wp": (n((N, M)) / np.sqrt(N) / v[:, None]).astype(np.float32),
        "gate": np.tile(np.random.uniform(0.2, 1.0, E * C), (N, 1)).astype(np.float32),
        "offs": striped(np.random.permutation(T)[:E * C]),
    }


def reference(xT, w_words, w_scales, b, wp, gate, offs):
    idx = unstriped(offs)
    w = np.stack([unpack_weight(w_words[e], w_scales[e], "e2m1") for e in range(E)])
    xq = mxq(f64(xT)[:, idx], 0, "e4m3")
    y = by_expert(w, xq)
    y = y + np.repeat(f64(b), C, axis=1)
    c = np.zeros((N, T))
    c[:, idx] = f64(gate) * y
    return mxq(f64(wp), 0, "e4m3").T @ mxq(c, 0, "e4m3")

@@ -1,0 +1,238 @@
+from contextlib import ExitStack
+
+import concourse.mybir as mybir
+from concourse.masks import make_identity
+
+K, T, E, C, N, M = 2560, 640, 2, 256, 512, 256
+P = 128
+S = E * C
+PASSES = K // 512
+TILES = S // P
+FT = M // P
+FLOPS = 2 * K * N * S + 2 * N * M * T
+BYTES = 4 * (K * T + N * E + N * M + S + M * T) + E * PASSES * (P * 1024 + 16 * N) + 256 * S // 16
+WORD_W = 688
+BYTE_W = 704
+
+F32 = mybir.dt.float32
+BF16 = mybir.dt.bfloat16
+I32 = mybir.dt.int32
+U32 = mybir.dt.uint32
+U16 = mybir.dt.uint16
+U8 = mybir.dt.uint8
+FP8X4 = mybir.dt.float8_e4m3fn_x4
+FP4X4 = mybir.dt.float4_e2m1fn_x4
+COPY = mybir.ActivationFunctionType.Copy
+MULT = mybir.AluOpType.mult
+ADD = mybir.AluOpType.add
+
+
+def tile_moe_nxt_lin_bias_kernel(tc, xT, w_words, w_scales, b, wp, gate, offs, out):
+    nc = tc.nc
+
+    def cast(engine, dst, src):
+        d = dst.rearrange("p (c i) j -> p c j i", i=4)
+        s = src.rearrange("p j (c i) -> p c j i", i=4)
+        if engine == "scalar":
+            nc.scalar.activation(out=d, in_=s, func=COPY)
+        else:
+            nc.vector.tensor_copy(d, s)
+
+    with ExitStack() as ctx:
+        keep = ctx.enter_context(tc.tile_pool(name="keep", bufs=1))
+        psum = ctx.enter_context(tc.psum_pool(name="psum", bufs=1))
+
+        offsets = keep.tile([P, S // 16], U16, name="offsets")
+        nc.sync.dma_start(offsets[:], offs)
+
+        x_chunks = {
+            0: [(0, 256), (256, 384)],
+            1: [(0, 640)],
+            2: [(0, 640)],
+            3: [(0, 640)],
+            4: [(0, 512), (512, 128)],
+        }
+        raw = {}
+
+        def load_x(a, i):
+            t0, n = x_chunks[a][i]
+            t = keep.tile([P, 4, n], F32, name=f"raw_{a}_{i}")
+            view = xT[512 * a : 512 * (a + 1), :].rearrange("(p j) t -> p j t", j=4)
+            nc.sync.dma_start(out=t[:], in_=view[:, :, t0 : t0 + n])
+            raw[(a, i)] = t
+
+        wq = [keep.tile([P, E, 2 * N], U8, name=f"wq_{a}", align_bytes=64) for a in range(PASSES)]
+
+        def load_w(a):
+            nc.sync.dma_start(
+                out=wq[a][:].bitcast(I32), in_=w_words[:, a, :, :].rearrange("e p c -> p e c").bitcast(I32)
+            )
+
+        b_raw = keep.tile([P, 4 * E], F32, name="b_raw")
+        gate_col = keep.tile([P, TILES], F32, name="gate_col")
+        nc.scalar.dma_start(out=b_raw[:], in_=b.rearrange("(p j) e -> p (j e)", j=4))
+        diagonal = gate.rearrange("n s -> (n s)")[0 : P * (S + 1)].rearrange("(p r) -> p r", r=S + 1)
+        with nc.allow_non_contiguous_dma(reason="one gate a partition"):
+            nc.scalar.dma_start(out=gate_col[:], in_=diagonal[:, 0:S:P])
+
+        wp_raw = keep.tile([P, 4, M], F32, name="wp_raw")
+        load_x(0, 0)
+        load_x(0, 1)
+        load_x(1, 0)
+        load_w(0)
+        load_x(2, 0)
+        load_x(3, 0)
+        load_w(1)
+        load_x(4, 0)
+        load_x(4, 1)
+        load_w(2)
+        load_w(3)
+        load_w(4)
+        nc.sync.dma_start(out=wp_raw[:], in_=wp.rearrange("(p j) f -> p j f", j=4))
+
+        ws = keep.tile([P, E * PASSES, N], U8, name="ws", align_bytes=64)
+        nc.vector.memset(ws[:].rearrange("p g n -> p (g n)").bitcast(I32), 0)
+        ws_src = w_scales.rearrange("e a (q r) n -> r q (e a) n", r=4)
+        for r in range(4):
+            nc.scalar.dma_start(out=ws[r:P:32, :, :].bitcast(I32), in_=ws_src[r].bitcast(I32))
+
+        words = [keep.tile([P, WORD_W], I32, name=f"words_{a}", align_bytes=64) for a in range(PASSES)]
+        scales = [keep.tile([P, BYTE_W], U8, name=f"scales_{a}", align_bytes=64) for a in range(PASSES)]
+        for a in range(PASSES):
+            nc.vector.memset(words[a][:, T:WORD_W], 0)
+            nc.gpsimd.memset(scales[a][:, T:BYTE_W], 0)
+
+        ident = keep.tile([P, P], F32, name="ident")
+        make_identity(nc, ident[:])
+        placed = [keep.tile([P, T], F32, name=f"placed_{f}") for f in range(FT)]
+
+        bias = [keep.tile([P, N], F32, name=f"bias_{e}") for e in range(E)]
+        gated_bias = [keep.tile([P, N], F32, name=f"gated_bias_{s}") for s in range(TILES)]
+        for e in range(E):
+            spread = psum.tile([P, 4, P], F32, name=f"spread_{e}", tag=f"turn_{e}")
+            for j in range(4):
+                nc.tensor.transpose(
+                    spread[:, j, :], b_raw[:, 2 * j + e : 2 * j + e + 1].to_broadcast([P, P]), ident[:]
+                )
+            nc.scalar.activation(
+                out=bias[e][:].rearrange("s (q j) -> s q j", j=4), in_=spread[:].rearrange("s j q -> s q j"), func=COPY
+            )
+        for s in range(TILES):
+            nc.gpsimd.tensor_scalar(
+                out=gated_bias[s][:], in0=bias[s // 2][:], scalar1=gate_col[:, s : s + 1], scalar2=0.0, op0=MULT, op1=ADD
+            )
+        for f in range(FT):
+            nc.gpsimd.memset(placed[f][:], 0.0)
+
+        xb = [keep.tile([P, T, 4], BF16, name=f"xb_{a}", align_bytes=64) for a in range(PASSES)]
+        slot_words = [keep.tile([P, S], U32, name=f"slot_words_{a}", align_bytes=64) for a in range(PASSES)]
+        slot_scales = [keep.tile([P, S], U8, name=f"slot_scales_{a}", align_bytes=64) for a in range(PASSES)]
+
+        def quantise(a, t0, n):
+            nc.vector.quantize_mx(
+                out=words[a][:, t0 : t0 + n].bitcast(FP8X4),
+                scales=scales[a][:, t0 : t0 + n],
+                in_=xb[a][:, t0 : t0 + n, :].rearrange("p t j -> p (t j)"),
+            )
+
+        def gather(a, s0, n):
+            lists = offsets[:] if n == S else offsets[:, s0 // 16 : (s0 + n) // 16]
+            nc.vector.tensor_copy(slot_words[a][:, s0 : s0 + n], words[a][:].bitcast(U32).indirect(lists))
+            nc.vector.tensor_copy(slot_scales[a][:, s0 : s0 + n], scales[a][:].indirect(lists))
+
+        y = [psum.tile([P, N], F32, name=f"y_{s}") for s in range(TILES)]
+
+        def multiply(a, s):
+            cols = slice(s * P, (s + 1) * P)
+            e = s // 2
+            nc.tensor.matmul_mx(
+                out=y[s][:],
+                lhsT=slot_words[a][:, cols].bitcast(FP8X4),
+                lhsT_scale=slot_scales[a][:, cols],
+                rhs=wq[a][:, e, :].bitcast(FP4X4),
+                rhs_scale=ws[:, e * PASSES + a, :],
+                start=(a == 0),
+                stop=(a == PASSES - 1),
+            )
+
+        wp_b = keep.tile([P, M, 4], BF16, name="wp_b", align_bytes=64)
+        wp_words = keep.tile([P, M], U32, name="wp_words", align_bytes=64)
+        wp_scales = keep.tile([P, M], U8, name="wp_scales", align_bytes=64)
+
+        for a in range(PASSES):
+            last = a == PASSES - 1
+            if a == 0:
+                pieces = [("vector", 0, 0, 256), ("scalar", 1, 0, 256), ("scalar", 1, 256, 128)]
+                widths = [(0, 256), (256, 256), (512, 128)]
+            elif last:
+                pieces = [("scalar", 0, 0, 512), ("vector", 1, 0, 128)]
+                widths = [(0, 512), (512, 128)]
+            else:
+                pieces = [("scalar", 0, 0, 512), ("scalar", 0, 512, 128)]
+                widths = [(0, 512), (512, 128)]
+            for engine, i, t0, n in pieces:
+                base = x_chunks[a][i][0]
+                cast(engine, xb[a][:, base + t0 : base + t0 + n, :], raw[(a, i)][:, :, t0 : t0 + n])
+            for t0, n in widths:
+                quantise(a, t0, n)
+            if a < PASSES - 2:
+                gather(a, 0, S)
+                for s in range(TILES):
+                    multiply(a, s)
+            else:
+                gather(a, 0, C)
+                multiply(a, 0)
+                multiply(a, 1)
+        for a in (PASSES - 2, PASSES - 1):
+            gather(a, C, C)
+            multiply(a, 2)
+            multiply(a, 3)
+
+        c_words = keep.tile([P, S], U32, name="c_words", align_bytes=64)
+        c_scales = keep.tile([P, S], U8, name="c_scales", align_bytes=64)
+        c = [keep.tile([P, N], BF16, name=f"c_{s}", align_bytes=64) for s in range(TILES)]
+        cT = [keep.tile([P, C, 4], BF16, name=f"cT_{e}", align_bytes=64) for e in range(E)]
+        z_sb = [keep.tile([P, FT, C], F32, name=f"z_sb_{e}") for e in range(E)]
+        for e in range(E):
+            for s in (2 * e, 2 * e + 1):
+                nc.vector.scalar_tensor_tensor(
+                    out=c[s][:], in0=y[s][:], scalar=gate_col[:, s : s + 1], in1=gated_bias[s][:], op0=MULT, op1=ADD
+                )
+            if e == 0:
+                cast("scalar", wp_b[:], wp_raw[:])
+                nc.vector.quantize_mx(
+                    out=wp_words[:].bitcast(FP8X4), scales=wp_scales[:], in_=wp_b[:].rearrange("p f j -> p (f j)")
+                )
+            turned = psum.tile([P, 2, 2, P], F32, name=f"turned_{e}", tag=f"turn_{e}")
+            for h in range(2):
+                pairs = c[2 * e + h][:].bitcast(F32)
+                for u in range(2):
+                    nc.tensor.transpose(turned[:, h, u, :], pairs[:, u : N // 2 : 2], ident[:])
+            nc.scalar.copy(
+                out=cT[e][:].rearrange("p (h r) j -> p h (r j)", h=2).bitcast(F32).rearrange("p h (r u) -> p h r u", u=2),
+                in_=turned[:].rearrange("p h u r -> p h r u"),
+            )
+            cols = slice(e * C, (e + 1) * C)
+            nc.vector.quantize_mx(
+                out=c_words[:, cols].bitcast(FP8X4), scales=c_scales[:, cols], in_=cT[e][:].rearrange("p s j -> p (s j)")
+            )
+            z = psum.tile([P, FT, C], F32, name=f"z_{e}")
+            for f in range(FT):
+                fcols = slice(f * P, (f + 1) * P)
+                nc.tensor.matmul_mx(
+                    out=z[:, f, :],
+                    lhsT=wp_words[:, fcols].bitcast(FP8X4),
+                    lhsT_scale=wp_scales[:, fcols],
+                    rhs=c_words[:, cols].bitcast(FP8X4),
+                    rhs_scale=c_scales[:, cols],
+                    start=True,
+                    stop=True,
+                )
+            for f in range(FT):
+                nc.scalar.activation(out=z_sb[e][:, f, :], in_=z[:, f, :], func=COPY)
+            for f in range(FT):
+                nc.vector.tensor_copy(
+                    placed[f][:].indirect(offsets[:, e * C // 16 : (e + 1) * C // 16]), z_sb[e][:, f, :]
+                )
+        for f in range(FT):
+            nc.sync.dma_start(out=out[f * P : (f + 1) * P, :], in_=placed[f][:])

@@ -45,29 +45,6 @@ def tile_moe_nxt_lin_bias_kernel(tc, xT, w_words, w_scales, b, wp, gate, offs, o
         offsets = keep.tile([P, S // 16], U16, name="offsets")
         nc.sync.dma_start(offsets[:], offs)
 
-        x_chunks = {
-            0: [(0, 256), (256, 384)],
-            1: [(0, 640)],
-            2: [(0, 640)],
-            3: [(0, 640)],
-            4: [(0, 512), (512, 128)],
-        }
-        raw = {}
-
-        def load_x(a, i):
-            t0, n = x_chunks[a][i]
-            t = keep.tile([P, 4, n], F32, name=f"raw_{a}_{i}")
-            view = xT[512 * a : 512 * (a + 1), :].rearrange("(p j) t -> p j t", j=4)
-            nc.sync.dma_start(out=t[:], in_=view[:, :, t0 : t0 + n])
-            raw[(a, i)] = t
-
-        wq = [keep.tile([P, E, 2 * N], U8, name=f"wq_{a}", align_bytes=64) for a in range(PASSES)]
-
-        def load_w(a):
-            nc.sync.dma_start(
-                out=wq[a][:].bitcast(I32), in_=w_words[:, a, :, :].rearrange("e p c -> p e c").bitcast(I32)
-            )
-
         b_raw = keep.tile([P, 4 * E], F32, name="b_raw")
         gate_col = keep.tile([P, TILES], F32, name="gate_col")
         nc.scalar.dma_start(out=b_raw[:], in_=b.rearrange("(p j) e -> p (j e)", j=4))
@@ -75,133 +52,152 @@ def tile_moe_nxt_lin_bias_kernel(tc, xT, w_words, w_scales, b, wp, gate, offs, o
         with nc.allow_non_contiguous_dma(reason="one gate a partition"):
             nc.scalar.dma_start(out=gate_col[:], in_=diagonal[:, 0:S:P])
 
+        chunks = {0: [(0, 256), (256, 384)], 1: [(0, 640)], 2: [(0, 640)], 3: [(0, 640)], 4: [(0, 512), (512, 128)]}
+        raw = {}
+        for a in range(PASSES):
+            view = xT[512 * a : 512 * (a + 1), :].rearrange("(p j) t -> p j t", j=4)
+            for t0, n in chunks[a]:
+                t = keep.tile([P, 4, n], F32, name=f"raw_{a}_{t0}")
+                nc.sync.dma_start(out=t[:], in_=view[:, :, t0 : t0 + n])
+                raw[(a, t0)] = t
+        wq = [keep.tile([P, PASSES, 2 * N], U8, name=f"wq_{e}", align_bytes=64) for e in range(E)]
         wp_raw = keep.tile([P, 4, M], F32, name="wp_raw")
-        load_x(0, 0)
-        load_x(0, 1)
-        load_x(1, 0)
-        load_w(0)
-        load_x(2, 0)
-        load_x(3, 0)
-        load_w(1)
-        load_x(4, 0)
-        load_x(4, 1)
-        load_w(2)
-        load_w(3)
-        load_w(4)
-        nc.sync.dma_start(out=wp_raw[:], in_=wp.rearrange("(p j) f -> p j f", j=4))
 
+        def load_w(e):
+            nc.sync.dma_start(out=wq[e][:].bitcast(I32), in_=w_words[e].rearrange("a p c -> p a c").bitcast(I32))
+
+        load_w(0)
+        nc.sync.dma_start(out=wp_raw[:], in_=wp.rearrange("(p j) f -> p j f", j=4))
+        load_w(1)
+
+        ident = keep.tile([P, P], F32, name="ident")
+        make_identity(nc, ident[:])
         ws = keep.tile([P, E * PASSES, N], U8, name="ws", align_bytes=64)
         nc.vector.memset(ws[:].rearrange("p g n -> p (g n)").bitcast(I32), 0)
         ws_src = w_scales.rearrange("e a (q r) n -> r q (e a) n", r=4)
         for r in range(4):
             nc.scalar.dma_start(out=ws[r:P:32, :, :].bitcast(I32), in_=ws_src[r].bitcast(I32))
-
         words = [keep.tile([P, WORD_W], I32, name=f"words_{a}", align_bytes=64) for a in range(PASSES)]
-        scales = [keep.tile([P, BYTE_W], U8, name=f"scales_{a}", align_bytes=64) for a in range(PASSES)]
         for a in range(PASSES):
             nc.vector.memset(words[a][:, T:WORD_W], 0)
-            nc.gpsimd.memset(scales[a][:, T:BYTE_W], 0)
 
-        ident = keep.tile([P, P], F32, name="ident")
-        make_identity(nc, ident[:])
+        packs = [(2, 0, 1), (3,), (4,)]
+        place = {}
+        plane = {}
+        slot_scales = {}
+        for g, members in enumerate(packs):
+            t = keep.tile([P, BYTE_W], U8, name=f"plane_{g}", align_bytes=64)
+            nc.gpsimd.memset(t[:, T:BYTE_W], 0)
+            for i, a in enumerate(members):
+                plane[a] = t
+                place[a] = 4 * i
+        slot_plane = [keep.tile([P, S], U8, name=f"slot_plane_{g}", align_bytes=64) for g in range(len(packs))]
+        for g, members in enumerate(packs):
+            slot_scales[members[0]] = slot_plane[g]
+            for a in members[1:]:
+                t = keep.tile([P, S], U8, name=f"slot_scales_{a}", align_bytes=64)
+                nc.gpsimd.memset(t[:].bitcast(I32), 0)
+                slot_scales[a] = t
         placed = [keep.tile([P, T], F32, name=f"placed_{f}") for f in range(FT)]
-
-        bias = [keep.tile([P, N], F32, name=f"bias_{e}") for e in range(E)]
-        gated_bias = [keep.tile([P, N], F32, name=f"gated_bias_{s}") for s in range(TILES)]
-        for e in range(E):
-            spread = psum.tile([P, 4, P], F32, name=f"spread_{e}", tag=f"turn_{e}")
-            for j in range(4):
-                nc.tensor.transpose(
-                    spread[:, j, :], b_raw[:, 2 * j + e : 2 * j + e + 1].to_broadcast([P, P]), ident[:]
-                )
-            nc.scalar.activation(
-                out=bias[e][:].rearrange("s (q j) -> s q j", j=4), in_=spread[:].rearrange("s j q -> s q j"), func=COPY
-            )
-        for s in range(TILES):
-            nc.gpsimd.tensor_scalar(
-                out=gated_bias[s][:], in0=bias[s // 2][:], scalar1=gate_col[:, s : s + 1], scalar2=0.0, op0=MULT, op1=ADD
-            )
         for f in range(FT):
             nc.gpsimd.memset(placed[f][:], 0.0)
 
+        gated_bias = [keep.tile([P, N], F32, name=f"gated_bias_{s}") for s in range(TILES)]
+
+        def spread_bias():
+            for e in range(E):
+                spread = psum.tile([P, 4, P], F32, name=f"spread_{e}", tag=f"turn_{e}")
+                for j in range(4):
+                    nc.tensor.transpose(
+                        spread[:, j, :], b_raw[:, 2 * j + e : 2 * j + e + 1].to_broadcast([P, P]), ident[:]
+                    )
+                for s in (2 * e, 2 * e + 1):
+                    nc.scalar.activation(
+                        out=gated_bias[s][:].rearrange("s (q j) -> s q j", j=4),
+                        in_=spread[:].rearrange("s j q -> s q j"),
+                        func=COPY,
+                        scale=gate_col[:, s : s + 1],
+                    )
+
         xb = [keep.tile([P, T, 4], BF16, name=f"xb_{a}", align_bytes=64) for a in range(PASSES)]
         slot_words = [keep.tile([P, S], U32, name=f"slot_words_{a}", align_bytes=64) for a in range(PASSES)]
-        slot_scales = [keep.tile([P, S], U8, name=f"slot_scales_{a}", align_bytes=64) for a in range(PASSES)]
+        pieces = {
+            0: [("vector", 0, 256), ("vector", 256, 384)],
+            1: [("scalar", 0, 256), ("vector", 256, 256), ("scalar", 512, 128)],
+            2: [("scalar", 0, 256), ("vector", 256, 256), ("scalar", 512, 128)],
+            3: [("scalar", 0, 512), ("vector", 512, 128)],
+            4: [("scalar", 0, 512), ("vector", 512, 128)],
+        }
+        widths = {0: [(0, 256), (256, 256), (512, 128)], 1: [(256, 256), (0, 256), (512, 128)], 2: [(256, 256), (0, 256), (512, 128)], 3: [(0, 512), (512, 128)], 4: [(0, 512), (512, 128)]}
 
-        def quantise(a, t0, n):
-            nc.vector.quantize_mx(
-                out=words[a][:, t0 : t0 + n].bitcast(FP8X4),
-                scales=scales[a][:, t0 : t0 + n],
-                in_=xb[a][:, t0 : t0 + n, :].rearrange("p t j -> p (t j)"),
-            )
+        def casts(a, which):
+            for engine, t0, n in pieces[a]:
+                if engine == which:
+                    c0 = [u for u, m in chunks[a] if u <= t0][-1]
+                    cast(engine, xb[a][:, t0 : t0 + n, :], raw[(a, c0)][:, :, t0 - c0 : t0 - c0 + n])
 
-        def gather(a, s0, n):
-            lists = offsets[:] if n == S else offsets[:, s0 // 16 : (s0 + n) // 16]
-            nc.vector.tensor_copy(slot_words[a][:, s0 : s0 + n], words[a][:].bitcast(U32).indirect(lists))
-            nc.vector.tensor_copy(slot_scales[a][:, s0 : s0 + n], scales[a][:].indirect(lists))
+        def quantise(a):
+            for t0, n in widths[a]:
+                nc.vector.quantize_mx(
+                    out=words[a][:, t0 : t0 + n].bitcast(FP8X4),
+                    scales=plane[a][place[a] : P, t0 : t0 + n],
+                    in_=xb[a][:, t0 : t0 + n, :].rearrange("p t j -> p (t j)"),
+                )
+
+        def slots(e):
+            return (slice(0, S), offsets[:]) if e is None else (slice(e * C, (e + 1) * C), offsets[:, e * C // 16 : (e + 1) * C // 16])
+
+        def gather_words(a, e):
+            cols, lists = slots(e)
+            nc.vector.tensor_copy(slot_words[a][:, cols], words[a][:].bitcast(U32).indirect(lists))
+
+        def gather_scales(g, e):
+            cols, lists = slots(e)
+            first = packs[g][0]
+            nc.vector.tensor_copy(slot_plane[g][:, cols], plane[first][:].indirect(lists))
+            for a in packs[g][1:]:
+                k = place[a]
+                nc.sync.dma_start(
+                    out=slot_scales[a][0 : P - k, cols].bitcast(I32), in_=slot_plane[g][k:P, cols].bitcast(I32)
+                )
 
         y = [psum.tile([P, N], F32, name=f"y_{s}") for s in range(TILES)]
+        order = (2, 0, 1, 3, 4)
 
-        def multiply(a, s):
-            cols = slice(s * P, (s + 1) * P)
-            e = s // 2
-            nc.tensor.matmul_mx(
-                out=y[s][:],
-                lhsT=slot_words[a][:, cols].bitcast(FP8X4),
-                lhsT_scale=slot_scales[a][:, cols],
-                rhs=wq[a][:, e, :].bitcast(FP4X4),
-                rhs_scale=ws[:, e * PASSES + a, :],
-                start=(a == 0),
-                stop=(a == PASSES - 1),
-            )
+        def multiply(e):
+            for a in order:
+                for s in (2 * e, 2 * e + 1):
+                    cols = slice(s * P, (s + 1) * P)
+                    nc.tensor.matmul_mx(
+                        out=y[s][:],
+                        lhsT=slot_words[a][:, cols].bitcast(FP8X4),
+                        lhsT_scale=slot_scales[a][:, cols],
+                        rhs=wq[e][:, a, :].bitcast(FP4X4),
+                        rhs_scale=ws[:, e * PASSES + a, :],
+                        start=(a == order[0]),
+                        stop=(a == order[-1]),
+                    )
 
         wp_b = keep.tile([P, M, 4], BF16, name="wp_b", align_bytes=64)
         wp_words = keep.tile([P, M], U32, name="wp_words", align_bytes=64)
         wp_scales = keep.tile([P, M], U8, name="wp_scales", align_bytes=64)
 
-        for a in range(PASSES):
-            last = a == PASSES - 1
-            if a == 0:
-                pieces = [("vector", 0, 0, 256), ("scalar", 1, 0, 256), ("scalar", 1, 256, 128)]
-                widths = [(0, 256), (256, 256), (512, 128)]
-            elif last:
-                pieces = [("scalar", 0, 0, 512), ("vector", 1, 0, 128)]
-                widths = [(0, 512), (512, 128)]
-            else:
-                pieces = [("scalar", 0, 0, 512), ("scalar", 0, 512, 128)]
-                widths = [(0, 512), (512, 128)]
-            for engine, i, t0, n in pieces:
-                base = x_chunks[a][i][0]
-                cast(engine, xb[a][:, base + t0 : base + t0 + n, :], raw[(a, i)][:, :, t0 : t0 + n])
-            for t0, n in widths:
-                quantise(a, t0, n)
-            if a < PASSES - 2:
-                gather(a, 0, S)
-                for s in range(TILES):
-                    multiply(a, s)
-            else:
-                gather(a, 0, C)
-                multiply(a, 0)
-                multiply(a, 1)
-        for a in (PASSES - 2, PASSES - 1):
-            gather(a, C, C)
-            multiply(a, 2)
-            multiply(a, 3)
+        def project_weights():
+            cast("scalar", wp_b[:], wp_raw[:])
+            nc.vector.quantize_mx(
+                out=wp_words[:].bitcast(FP8X4), scales=wp_scales[:], in_=wp_b[:].rearrange("p f j -> p (f j)")
+            )
 
         c_words = keep.tile([P, S], U32, name="c_words", align_bytes=64)
         c_scales = keep.tile([P, S], U8, name="c_scales", align_bytes=64)
         c = [keep.tile([P, N], BF16, name=f"c_{s}", align_bytes=64) for s in range(TILES)]
         cT = [keep.tile([P, C, 4], BF16, name=f"cT_{e}", align_bytes=64) for e in range(E)]
         z_sb = [keep.tile([P, FT, C], F32, name=f"z_sb_{e}") for e in range(E)]
-        for e in range(E):
+
+        def finish(e):
             for s in (2 * e, 2 * e + 1):
                 nc.vector.scalar_tensor_tensor(
                     out=c[s][:], in0=y[s][:], scalar=gate_col[:, s : s + 1], in1=gated_bias[s][:], op0=MULT, op1=ADD
-                )
-            if e == 0:
-                cast("scalar", wp_b[:], wp_raw[:])
-                nc.vector.quantize_mx(
-                    out=wp_words[:].bitcast(FP8X4), scales=wp_scales[:], in_=wp_b[:].rearrange("p f j -> p (f j)")
                 )
             turned = psum.tile([P, 2, 2, P], F32, name=f"turned_{e}", tag=f"turn_{e}")
             for h in range(2):
@@ -230,9 +226,45 @@ def tile_moe_nxt_lin_bias_kernel(tc, xT, w_words, w_scales, b, wp, gate, offs, o
                 )
             for f in range(FT):
                 nc.scalar.activation(out=z_sb[e][:, f, :], in_=z[:, f, :], func=COPY)
+
+        def scatter(e):
             for f in range(FT):
-                nc.vector.tensor_copy(
-                    placed[f][:].indirect(offsets[:, e * C // 16 : (e + 1) * C // 16]), z_sb[e][:, f, :]
-                )
+                nc.vector.tensor_copy(placed[f][:].indirect(slots(e)[1]), z_sb[e][:, f, :])
+
+        spread_bias()
+        casts(0, "scalar")
+        casts(0, "vector")
+        quantise(0)
+        casts(1, "scalar")
+        casts(1, "vector")
+        gather_words(0, None)
+        quantise(1)
+        casts(2, "scalar")
+        casts(2, "vector")
+        gather_words(1, None)
+        quantise(2)
+        casts(3, "scalar")
+        casts(3, "vector")
+        gather_scales(0, None)
+        gather_words(2, None)
+        quantise(3)
+        casts(4, "scalar")
+        casts(4, "vector")
+        gather_words(3, 0)
+        gather_scales(1, 0)
+        quantise(4)
+        gather_words(4, 0)
+        gather_scales(2, 0)
+        multiply(0)
+        project_weights()
+        finish(0)
+        gather_words(3, 1)
+        gather_scales(1, 1)
+        gather_words(4, 1)
+        gather_scales(2, 1)
+        multiply(1)
+        finish(1)
+        scatter(0)
+        scatter(1)
         for f in range(FT):
             nc.sync.dma_start(out=out[f * P : (f + 1) * P, :], in_=placed[f][:])

@@ -42,6 +42,11 @@ def tile_moe_nxt_lin_bias_kernel(tc, xT, w_words, w_scales, b, wp, gate, offs, o
         keep = ctx.enter_context(tc.tile_pool(name="keep", bufs=1))
         psum = ctx.enter_context(tc.psum_pool(name="psum", bufs=1))
 
+        probe = keep.tile([P, 1], F32, name="probe")
+        nc.gpsimd.memset(probe[:], 0.0)
+        probe_out = keep.tile([P, 1], F32, name="probe_out")
+        nc.scalar.activation(out=probe_out[:], in_=probe[:], func=COPY)
+
         offsets = keep.tile([P, S // 16], U16, name="offsets")
         nc.sync.dma_start(offsets[:], offs)
 
@@ -54,21 +59,30 @@ def tile_moe_nxt_lin_bias_kernel(tc, xT, w_words, w_scales, b, wp, gate, offs, o
 
         chunks = {0: [(0, 256), (256, 384)], 1: [(0, 640)], 2: [(0, 640)], 3: [(0, 640)], 4: [(0, 512), (512, 128)]}
         raw = {}
-        for a in range(PASSES):
+
+        def load_x(a):
             view = xT[512 * a : 512 * (a + 1), :].rearrange("(p j) t -> p j t", j=4)
             for t0, n in chunks[a]:
                 t = keep.tile([P, 4, n], F32, name=f"raw_{a}_{t0}")
                 nc.sync.dma_start(out=t[:], in_=view[:, :, t0 : t0 + n])
                 raw[(a, t0)] = t
+
         wq = [keep.tile([P, PASSES, 2 * N], U8, name=f"wq_{e}", align_bytes=64) for e in range(E)]
         wp_raw = keep.tile([P, 4, M], F32, name="wp_raw")
 
-        def load_w(e):
-            nc.sync.dma_start(out=wq[e][:].bitcast(I32), in_=w_words[e].rearrange("a p c -> p a c").bitcast(I32))
+        def load_w(e, a0, a1):
+            nc.sync.dma_start(
+                out=wq[e][:, a0:a1, :].bitcast(I32), in_=w_words[e, a0:a1, :, :].rearrange("a p c -> p a c").bitcast(I32)
+            )
 
-        load_w(0)
-        nc.sync.dma_start(out=wp_raw[:], in_=wp.rearrange("(p j) f -> p j f", j=4))
-        load_w(1)
+        def load_wp():
+            nc.sync.dma_start(out=wp_raw[:], in_=wp.rearrange("(p j) f -> p j f", j=4))
+
+        for a in range(PASSES):
+            load_x(a)
+        load_w(0, 0, 5)
+        load_wp()
+        load_w(1, 0, 5)
 
         ident = keep.tile([P, P], F32, name="ident")
         make_identity(nc, ident[:])
@@ -81,7 +95,7 @@ def tile_moe_nxt_lin_bias_kernel(tc, xT, w_words, w_scales, b, wp, gate, offs, o
         for a in range(PASSES):
             nc.vector.memset(words[a][:, T:WORD_W], 0)
 
-        packs = [(2, 0, 1), (3,), (4,)]
+        packs = [(1, 0), (2,), (3,), (4,)]
         place = {}
         plane = {}
         slot_scales = {}
@@ -91,13 +105,17 @@ def tile_moe_nxt_lin_bias_kernel(tc, xT, w_words, w_scales, b, wp, gate, offs, o
             for i, a in enumerate(members):
                 plane[a] = t
                 place[a] = 4 * i
-        slot_plane = [keep.tile([P, S], U8, name=f"slot_plane_{g}", align_bytes=64) for g in range(len(packs))]
         for g, members in enumerate(packs):
-            slot_scales[members[0]] = slot_plane[g]
-            for a in members[1:]:
-                t = keep.tile([P, S], U8, name=f"slot_scales_{a}", align_bytes=64)
-                nc.gpsimd.memset(t[:].bitcast(I32), 0)
-                slot_scales[a] = t
+            for a in members:
+                split = members[0] in (3, 4)
+                for e in range(E) if split else (None,):
+                    t = keep.tile([P, C if split else S], U8, name=f"slot_scales_{a}_{e}", align_bytes=64)
+                    if a != members[0]:
+                        nc.gpsimd.memset(t[:].bitcast(I32), 0)
+                    slot_scales[(a, e)] = t[:]
+                if not split:
+                    for e in range(E):
+                        slot_scales[(a, e)] = slot_scales[(a, None)][:, e * C : (e + 1) * C]
         placed = [keep.tile([P, T], F32, name=f"placed_{f}") for f in range(FT)]
         for f in range(FT):
             nc.gpsimd.memset(placed[f][:], 0.0)
@@ -120,15 +138,25 @@ def tile_moe_nxt_lin_bias_kernel(tc, xT, w_words, w_scales, b, wp, gate, offs, o
                     )
 
         xb = [keep.tile([P, T, 4], BF16, name=f"xb_{a}", align_bytes=64) for a in range(PASSES)]
-        slot_words = [keep.tile([P, S], U32, name=f"slot_words_{a}", align_bytes=64) for a in range(PASSES)]
+        halves = (3, 4)
+        slot_words = {}
+        for a in range(PASSES):
+            for e in range(E):
+                if a in halves:
+                    slot_words[(a, e)] = keep.tile([P, C], U32, name=f"slot_words_{a}_{e}", align_bytes=64)[:]
+            if a not in halves:
+                whole = keep.tile([P, S], U32, name=f"slot_words_{a}", align_bytes=64)
+                slot_words[(a, None)] = whole[:]
+                for e in range(E):
+                    slot_words[(a, e)] = whole[:, e * C : (e + 1) * C]
         pieces = {
-            0: [("vector", 0, 256), ("vector", 256, 384)],
-            1: [("scalar", 0, 256), ("vector", 256, 256), ("scalar", 512, 128)],
-            2: [("scalar", 0, 256), ("vector", 256, 256), ("scalar", 512, 128)],
-            3: [("scalar", 0, 512), ("vector", 512, 128)],
-            4: [("scalar", 0, 512), ("vector", 512, 128)],
+            0: [("vector", 0, 256), ("scalar", 256, 384)],
+            1: [("scalar", 0, 512), ("scalar", 512, 128)],
+            2: [("scalar", 0, 512), ("scalar", 512, 128)],
+            3: [("scalar", 0, 512), ("scalar", 512, 128)],
+            4: [("scalar", 0, 256), ("vector", 256, 256), ("vector", 512, 128)],
         }
-        widths = {0: [(0, 256), (256, 256), (512, 128)], 1: [(256, 256), (0, 256), (512, 128)], 2: [(256, 256), (0, 256), (512, 128)], 3: [(0, 512), (512, 128)], 4: [(0, 512), (512, 128)]}
+        widths = {0: [(0, 256), (256, 256), (512, 128)], 1: [(0, 512), (512, 128)], 2: [(0, 512), (512, 128)], 3: [(0, 512), (512, 128)], 4: [(256, 256), (512, 128), (0, 256)]}
 
         def casts(a, which):
             for engine, t0, n in pieces[a]:
@@ -148,30 +176,30 @@ def tile_moe_nxt_lin_bias_kernel(tc, xT, w_words, w_scales, b, wp, gate, offs, o
             return (slice(0, S), offsets[:]) if e is None else (slice(e * C, (e + 1) * C), offsets[:, e * C // 16 : (e + 1) * C // 16])
 
         def gather_words(a, e):
-            cols, lists = slots(e)
-            nc.vector.tensor_copy(slot_words[a][:, cols], words[a][:].bitcast(U32).indirect(lists))
+            lists = slots(e)[1]
+            nc.vector.tensor_copy(slot_words[(a, e)], words[a][:].bitcast(U32).indirect(lists))
 
         def gather_scales(g, e):
-            cols, lists = slots(e)
+            lists = slots(e)[1]
             first = packs[g][0]
-            nc.vector.tensor_copy(slot_plane[g][:, cols], plane[first][:].indirect(lists))
+            nc.vector.tensor_copy(slot_scales[(first, e)], plane[first][:].indirect(lists))
             for a in packs[g][1:]:
                 k = place[a]
                 nc.sync.dma_start(
-                    out=slot_scales[a][0 : P - k, cols].bitcast(I32), in_=slot_plane[g][k:P, cols].bitcast(I32)
+                    out=slot_scales[(a, e)][0 : P - k, :].bitcast(I32), in_=slot_scales[(first, e)][k:P, :].bitcast(I32)
                 )
 
         y = [psum.tile([P, N], F32, name=f"y_{s}") for s in range(TILES)]
-        order = (2, 0, 1, 3, 4)
+        order = (1, 2, 3, 0, 4)
 
-        def multiply(e):
-            for a in order:
+        def multiply(e, passes):
+            for a in passes:
                 for s in (2 * e, 2 * e + 1):
-                    cols = slice(s * P, (s + 1) * P)
+                    cols = slice((s - 2 * e) * P, (s - 2 * e + 1) * P)
                     nc.tensor.matmul_mx(
                         out=y[s][:],
-                        lhsT=slot_words[a][:, cols].bitcast(FP8X4),
-                        lhsT_scale=slot_scales[a][:, cols],
+                        lhsT=slot_words[(a, e)][:, cols].bitcast(FP8X4),
+                        lhsT_scale=slot_scales[(a, e)][:, cols],
                         rhs=wq[e][:, a, :].bitcast(FP4X4),
                         rhs_scale=ws[:, e * PASSES + a, :],
                         start=(a == order[0]),
@@ -191,32 +219,40 @@ def tile_moe_nxt_lin_bias_kernel(tc, xT, w_words, w_scales, b, wp, gate, offs, o
         c_words = keep.tile([P, S], U32, name="c_words", align_bytes=64)
         c_scales = keep.tile([P, S], U8, name="c_scales", align_bytes=64)
         c = [keep.tile([P, N], BF16, name=f"c_{s}", align_bytes=64) for s in range(TILES)]
-        cT = [keep.tile([P, C, 4], BF16, name=f"cT_{e}", align_bytes=64) for e in range(E)]
-        z_sb = [keep.tile([P, FT, C], F32, name=f"z_sb_{e}") for e in range(E)]
+        cT = [keep.tile([P, P, 4], BF16, name=f"cT_{s}", align_bytes=64) for s in range(TILES)]
+        z_sb = [keep.tile([P, FT, P], F32, name=f"z_sb_{s}") for s in range(TILES)]
+        turned = {}
+        z = {}
 
-        def finish(e):
-            for s in (2 * e, 2 * e + 1):
-                nc.vector.scalar_tensor_tensor(
-                    out=c[s][:], in0=y[s][:], scalar=gate_col[:, s : s + 1], in1=gated_bias[s][:], op0=MULT, op1=ADD
-                )
-            turned = psum.tile([P, 2, 2, P], F32, name=f"turned_{e}", tag=f"turn_{e}")
-            for h in range(2):
-                pairs = c[2 * e + h][:].bitcast(F32)
-                for u in range(2):
-                    nc.tensor.transpose(turned[:, h, u, :], pairs[:, u : N // 2 : 2], ident[:])
+        def evacuate(s):
+            nc.vector.scalar_tensor_tensor(
+                out=c[s][:], in0=y[s][:], scalar=gate_col[:, s : s + 1], in1=gated_bias[s][:], op0=MULT, op1=ADD
+            )
+
+        def turn(s):
+            e, h = divmod(s, 2)
+            if h == 0:
+                turned[e] = psum.tile([P, 2, 2, P], F32, name=f"turned_{e}", tag=f"turn_{e}")
+            pairs = c[s][:].bitcast(F32)
+            for u in range(2):
+                nc.tensor.transpose(turned[e][:, h, u, :], pairs[:, u : N // 2 : 2], ident[:])
             nc.scalar.copy(
-                out=cT[e][:].rearrange("p (h r) j -> p h (r j)", h=2).bitcast(F32).rearrange("p h (r u) -> p h r u", u=2),
-                in_=turned[:].rearrange("p h u r -> p h r u"),
+                out=cT[s][:].rearrange("p r j -> p (r j)").bitcast(F32).rearrange("p (r u) -> p r u", u=2),
+                in_=turned[e][:, h, :, :].rearrange("p u r -> p r u"),
             )
-            cols = slice(e * C, (e + 1) * C)
+
+        def project(s):
+            e, h = divmod(s, 2)
+            cols = slice(s * P, (s + 1) * P)
             nc.vector.quantize_mx(
-                out=c_words[:, cols].bitcast(FP8X4), scales=c_scales[:, cols], in_=cT[e][:].rearrange("p s j -> p (s j)")
+                out=c_words[:, cols].bitcast(FP8X4), scales=c_scales[:, cols], in_=cT[s][:].rearrange("p r j -> p (r j)")
             )
-            z = psum.tile([P, FT, C], F32, name=f"z_{e}")
+            if h == 0:
+                z[e] = psum.tile([P, 2, FT, P], F32, name=f"z_{e}")
             for f in range(FT):
                 fcols = slice(f * P, (f + 1) * P)
                 nc.tensor.matmul_mx(
-                    out=z[:, f, :],
+                    out=z[e][:, h, f, :],
                     lhsT=wp_words[:, fcols].bitcast(FP8X4),
                     lhsT_scale=wp_scales[:, fcols],
                     rhs=c_words[:, cols].bitcast(FP8X4),
@@ -224,14 +260,12 @@ def tile_moe_nxt_lin_bias_kernel(tc, xT, w_words, w_scales, b, wp, gate, offs, o
                     start=True,
                     stop=True,
                 )
-            for f in range(FT):
-                nc.scalar.activation(out=z_sb[e][:, f, :], in_=z[:, f, :], func=COPY)
+            nc.scalar.activation(out=z_sb[s][:], in_=z[e][:, h, :, :], func=COPY)
 
-        def scatter(e):
+        def scatter(s):
             for f in range(FT):
-                nc.vector.tensor_copy(placed[f][:].indirect(slots(e)[1]), z_sb[e][:, f, :])
+                nc.vector.tensor_copy(placed[f][:].indirect(offsets[:, s * P // 16 : (s + 1) * P // 16]), z_sb[s][:, f, :])
 
-        spread_bias()
         casts(0, "scalar")
         casts(0, "vector")
         quantise(0)
@@ -239,32 +273,37 @@ def tile_moe_nxt_lin_bias_kernel(tc, xT, w_words, w_scales, b, wp, gate, offs, o
         casts(1, "vector")
         gather_words(0, None)
         quantise(1)
+        gather_scales(0, None)
+        gather_words(1, None)
         casts(2, "scalar")
         casts(2, "vector")
-        gather_words(1, None)
         quantise(2)
         casts(3, "scalar")
         casts(3, "vector")
-        gather_scales(0, None)
         gather_words(2, None)
+        gather_scales(1, None)
         quantise(3)
         casts(4, "scalar")
         casts(4, "vector")
+        spread_bias()
         gather_words(3, 0)
-        gather_scales(1, 0)
+        gather_scales(2, 0)
         quantise(4)
         gather_words(4, 0)
-        gather_scales(2, 0)
-        multiply(0)
-        project_weights()
-        finish(0)
+        gather_scales(3, 0)
         gather_words(3, 1)
-        gather_scales(1, 1)
-        gather_words(4, 1)
         gather_scales(2, 1)
-        multiply(1)
-        finish(1)
-        scatter(0)
-        scatter(1)
+        gather_words(4, 1)
+        gather_scales(3, 1)
+        multiply(0, order)
+        project_weights()
+        multiply(1, order)
+        for s in range(TILES):
+            evacuate(s)
+            turn(s)
+        for s in range(TILES):
+            project(s)
+        for s in range(TILES):
+            scatter(s)
         for f in range(FT):
             nc.sync.dma_start(out=out[f * P : (f + 1) * P, :], in_=placed[f][:])

@@ -5,14 +5,39 @@ from concourse.masks import make_identity
 
 K, T, E, C, N, M = 2560, 640, 2, 256, 512, 256
 P = 128
+PACK = 4
+PASSES = K // (P * PACK)
 S = E * C
-PASSES = K // 512
 TILES = S // P
 FT = M // P
+LIST = 16
+
+WORD_COLUMNS = 688
+BYTE_COLUMNS = 704
+
+SHARED_ROW = 4
+
+LOADS = (((0, 256), (256, 384)), ((0, 640),), ((0, 640),), ((0, 640),), ((0, 512), (512, 128)))
+CASTS = (
+    (("vector", 0, 256), ("vector", 256, 384)),
+    (("scalar", 256, 256), ("vector", 0, 256), ("vector", 512, 128)),
+    (("scalar", 0, 512), ("vector", 512, 128)),
+    (("scalar", 0, 512), ("scalar", 512, 128)),
+    (("scalar", 0, 256), ("scalar", 256, 256), ("scalar", 512, 128)),
+)
+QUANTISED = (
+    ((0, 256), (256, 256), (512, 128)),
+    ((0, 256), (512, 128), (256, 256)),
+    ((512, 128), (0, 512)),
+    ((0, 512), (512, 128)),
+    ((0, 256), (256, 256), (512, 128)),
+)
+WHOLE_PASSES = (0, 1, 2)
+SPLIT_PASSES = (3, 4)
+ORDER = (1, 2, 3, 0, 4)
+
 FLOPS = 2 * K * N * S + 2 * N * M * T
-BYTES = 4 * (K * T + N * E + N * M + S + M * T) + E * PASSES * (P * 1024 + 16 * N) + 256 * S // 16
-WORD_W = 688
-BYTE_W = 704
+BYTES = 4 * (K * T + N * E + N * M + S + M * T) + E * PASSES * (2 * P * N + 16 * N) + 2 * P * S // LIST
 
 F32 = mybir.dt.float32
 BF16 = mybir.dt.bfloat16
@@ -30,280 +55,247 @@ ADD = mybir.AluOpType.add
 def tile_moe_nxt_lin_bias_kernel(tc, xT, w_words, w_scales, b, wp, gate, offs, out):
     nc = tc.nc
 
-    def cast(engine, dst, src):
-        d = dst.rearrange("p (c i) j -> p c j i", i=4)
-        s = src.rearrange("p j (c i) -> p c j i", i=4)
+    def round_and_interleave(engine, dst, src):
+        dst = dst.rearrange("p (c i) j -> p c j i", i=4)
+        src = src.rearrange("p j (c i) -> p c j i", i=4)
         if engine == "scalar":
-            nc.scalar.activation(out=d, in_=s, func=COPY)
+            nc.scalar.activation(out=dst, in_=src, func=COPY)
         else:
-            nc.vector.tensor_copy(d, s)
+            nc.vector.tensor_copy(dst, src)
 
     with ExitStack() as ctx:
         keep = ctx.enter_context(tc.tile_pool(name="keep", bufs=1))
         psum = ctx.enter_context(tc.psum_pool(name="psum", bufs=1))
 
-        probe = keep.tile([P, 1], F32, name="probe")
-        nc.gpsimd.memset(probe[:], 0.0)
-        probe_out = keep.tile([P, 1], F32, name="probe_out")
-        nc.scalar.activation(out=probe_out[:], in_=probe[:], func=COPY)
+        early = keep.tile([P, 1], F32, name="early")
+        nc.gpsimd.memset(early[:], 0.0)
+        early_copy = keep.tile([P, 1], F32, name="early_copy")
+        nc.scalar.activation(out=early_copy[:], in_=early[:], func=COPY)
 
-        offsets = keep.tile([P, S // 16], U16, name="offsets")
-        nc.sync.dma_start(offsets[:], offs)
+        offsets = keep.tile([P, S // LIST], U16, name="offsets")
+        bias_rows = keep.tile([P, PACK * E], F32, name="bias_rows")
+        gate_column = keep.tile([P, TILES], F32, name="gate_column")
+        w_bytes = keep.tile([P, E * PASSES, N], U8, name="w_bytes", align_bytes=64)
+        w_codes = [keep.tile([P, PASSES, 2 * N], U8, name=f"w_codes_{e}", align_bytes=64) for e in range(E)]
+        wp_raw = keep.tile([P, PACK, M], F32, name="wp_raw")
+        x_raw = {}
 
-        b_raw = keep.tile([P, 4 * E], F32, name="b_raw")
-        gate_col = keep.tile([P, TILES], F32, name="gate_col")
-        nc.scalar.dma_start(out=b_raw[:], in_=b.rearrange("(p j) e -> p (j e)", j=4))
-        diagonal = gate.rearrange("n s -> (n s)")[0 : P * (S + 1)].rearrange("(p r) -> p r", r=S + 1)
-        with nc.allow_non_contiguous_dma(reason="one gate a partition"):
-            nc.scalar.dma_start(out=gate_col[:], in_=diagonal[:, 0:S:P])
-
-        chunks = {0: [(0, 256), (256, 384)], 1: [(0, 640)], 2: [(0, 640)], 3: [(0, 640)], 4: [(0, 512), (512, 128)]}
-        raw = {}
-
-        def load_x(a):
-            view = xT[512 * a : 512 * (a + 1), :].rearrange("(p j) t -> p j t", j=4)
-            for t0, n in chunks[a]:
-                t = keep.tile([P, 4, n], F32, name=f"raw_{a}_{t0}")
-                nc.sync.dma_start(out=t[:], in_=view[:, :, t0 : t0 + n])
-                raw[(a, t0)] = t
-
-        wq = [keep.tile([P, PASSES, 2 * N], U8, name=f"wq_{e}", align_bytes=64) for e in range(E)]
-        wp_raw = keep.tile([P, 4, M], F32, name="wp_raw")
-
-        def load_w(e, a0, a1):
-            nc.sync.dma_start(
-                out=wq[e][:, a0:a1, :].bitcast(I32), in_=w_words[e, a0:a1, :, :].rearrange("a p c -> p a c").bitcast(I32)
-            )
-
-        def load_wp():
-            nc.sync.dma_start(out=wp_raw[:], in_=wp.rearrange("(p j) f -> p j f", j=4))
+        nc.vector.memset(w_bytes[:].rearrange("p g n -> p (g n)").bitcast(I32), 0)
 
         for a in range(PASSES):
-            load_x(a)
-        load_w(0, 0, 5)
-        load_wp()
-        load_w(1, 0, 5)
+            rows = xT[P * PACK * a : P * PACK * (a + 1), :].rearrange("(p j) t -> p j t", j=PACK)
+            for t0, n in LOADS[a]:
+                piece = keep.tile([P, PACK, n], F32, name=f"x_raw_{a}_{t0}")
+                nc.sync.dma_start(out=piece[:], in_=rows[:, :, t0 : t0 + n])
+                x_raw[(a, t0)] = piece
+                if (a, t0) == (0, 0):
+                    nc.sync.dma_start(offsets[:], offs)
+            if a == 1:
+                nc.sync.dma_start(out=bias_rows[:], in_=b.rearrange("(p j) e -> p (j e)", j=PACK))
+                diagonal = gate.rearrange("n s -> (n s)")[0 : P * (S + 1)].rearrange("(p r) -> p r", r=S + 1)
+                with nc.allow_non_contiguous_dma(reason="one gate a partition"):
+                    nc.sync.dma_start(out=gate_column[:], in_=diagonal[:, 0:S:P])
 
-        ident = keep.tile([P, P], F32, name="ident")
-        make_identity(nc, ident[:])
-        ws = keep.tile([P, E * PASSES, N], U8, name="ws", align_bytes=64)
-        nc.vector.memset(ws[:].rearrange("p g n -> p (g n)").bitcast(I32), 0)
-        ws_src = w_scales.rearrange("e a (q r) n -> r q (e a) n", r=4)
+        byte_rows = w_scales.rearrange("e a (q r) n -> r q (e a) n", r=4)
         for r in range(4):
-            nc.scalar.dma_start(out=ws[r:P:32, :, :].bitcast(I32), in_=ws_src[r].bitcast(I32))
-        words = [keep.tile([P, WORD_W], I32, name=f"words_{a}", align_bytes=64) for a in range(PASSES)]
-        for a in range(PASSES):
-            nc.vector.memset(words[a][:, T:WORD_W], 0)
+            nc.sync.dma_start(out=w_bytes[r:P:32, :, :].bitcast(I32), in_=byte_rows[r].bitcast(I32))
 
-        packs = [(1, 0), (2,), (3,), (4,)]
-        place = {}
-        plane = {}
-        slot_scales = {}
-        for g, members in enumerate(packs):
-            t = keep.tile([P, BYTE_W], U8, name=f"plane_{g}", align_bytes=64)
-            nc.gpsimd.memset(t[:, T:BYTE_W], 0)
-            for i, a in enumerate(members):
-                plane[a] = t
-                place[a] = 4 * i
-        for g, members in enumerate(packs):
-            for a in members:
-                split = members[0] in (3, 4)
-                for e in range(E) if split else (None,):
-                    t = keep.tile([P, C if split else S], U8, name=f"slot_scales_{a}_{e}", align_bytes=64)
-                    if a != members[0]:
-                        nc.gpsimd.memset(t[:].bitcast(I32), 0)
-                    slot_scales[(a, e)] = t[:]
-                if not split:
-                    for e in range(E):
-                        slot_scales[(a, e)] = slot_scales[(a, None)][:, e * C : (e + 1) * C]
-        placed = [keep.tile([P, T], F32, name=f"placed_{f}") for f in range(FT)]
+        def load_expert(e):
+            nc.sync.dma_start(out=w_codes[e][:].bitcast(I32), in_=w_words[e].rearrange("a p c -> p a c").bitcast(I32))
+
+        load_expert(0)
+        nc.sync.dma_start(out=wp_raw[:], in_=wp.rearrange("(p j) f -> p j f", j=PACK))
+        load_expert(1)
+
+        identity = keep.tile([P, P], F32, name="identity")
+        make_identity(nc, identity[:])
+
+        words = [keep.tile([P, WORD_COLUMNS], I32, name=f"words_{a}", align_bytes=64) for a in range(PASSES)]
+        for a in range(PASSES):
+            nc.vector.memset(words[a][:, T:WORD_COLUMNS], 0)
+        scales = {}
+        for a in range(1, PASSES):
+            scales[a] = keep.tile([P, BYTE_COLUMNS], U8, name=f"scales_{a}", align_bytes=64)
+            nc.gpsimd.memset(scales[a][:, T:BYTE_COLUMNS], 0)
+        scales[0] = scales[1]
+
+        slot_words, slot_scales = {}, {}
+        for a in WHOLE_PASSES:
+            words_tile = keep.tile([P, S], U32, name=f"slot_words_{a}", align_bytes=64)
+            bytes_tile = keep.tile([P, S], U8, name=f"slot_scales_{a}", align_bytes=64)
+            slot_words[(a, "all")], slot_scales[(a, "all")] = words_tile[:], bytes_tile[:]
+            for e in range(E):
+                slot_words[(a, e)] = words_tile[:, e * C : (e + 1) * C]
+                slot_scales[(a, e)] = bytes_tile[:, e * C : (e + 1) * C]
+        for a in SPLIT_PASSES:
+            for e in range(E):
+                words_tile = keep.tile([P, C], U32, name=f"slot_words_{a}_{e}", align_bytes=64)
+                bytes_tile = keep.tile([P, C], U8, name=f"slot_scales_{a}_{e}", align_bytes=64)
+                slot_words[(a, e)], slot_scales[(a, e)] = words_tile[:], bytes_tile[:]
+        nc.gpsimd.memset(slot_scales[(0, "all")].bitcast(I32), 0)
+
+        out_tile = [keep.tile([P, T], F32, name=f"out_tile_{f}") for f in range(FT)]
         for f in range(FT):
-            nc.gpsimd.memset(placed[f][:], 0.0)
+            nc.gpsimd.memset(out_tile[f][:], 0.0)
+
+        x_rounded = [keep.tile([P, T, PACK], BF16, name=f"x_rounded_{a}", align_bytes=64) for a in range(PASSES)]
+
+        def round_tokens(a):
+            for engine, t0, n in CASTS[a]:
+                start = max(u for u, count in LOADS[a] if u <= t0)
+                round_and_interleave(
+                    engine, x_rounded[a][:, t0 : t0 + n, :], x_raw[(a, start)][:, :, t0 - start : t0 - start + n]
+                )
+
+        def quantise_tokens(a):
+            row = SHARED_ROW if a == 0 else 0
+            for t0, n in QUANTISED[a]:
+                nc.vector.quantize_mx(
+                    out=words[a][:, t0 : t0 + n].bitcast(FP8X4),
+                    scales=scales[a][row:P, t0 : t0 + n],
+                    in_=x_rounded[a][:, t0 : t0 + n, :].rearrange("p t j -> p (t j)"),
+                )
+
+        def slot_list(e):
+            return offsets[:] if e == "all" else offsets[:, e * C // LIST : (e + 1) * C // LIST]
+
+        def gather_words(a, e):
+            nc.vector.tensor_copy(slot_words[(a, e)], words[a][:].bitcast(U32).indirect(slot_list(e)))
+
+        def gather_scales(a, e):
+            nc.vector.tensor_copy(slot_scales[(a, e)], scales[a][:].indirect(slot_list(e)))
+
+        y = [psum.tile([P, N], F32, name=f"y_{s}") for s in range(TILES)]
+
+        def multiply(e):
+            for a in ORDER:
+                for h in range(2):
+                    slots = slice(h * P, (h + 1) * P)
+                    nc.tensor.matmul_mx(
+                        out=y[2 * e + h][:],
+                        lhsT=slot_words[(a, e)][:, slots].bitcast(FP8X4),
+                        lhsT_scale=slot_scales[(a, e)][:, slots],
+                        rhs=w_codes[e][:, a, :].bitcast(FP4X4),
+                        rhs_scale=w_bytes[:, e * PASSES + a, :],
+                        start=(a == ORDER[0]),
+                        stop=(a == ORDER[-1]),
+                    )
 
         gated_bias = [keep.tile([P, N], F32, name=f"gated_bias_{s}") for s in range(TILES)]
 
         def spread_bias():
             for e in range(E):
-                spread = psum.tile([P, 4, P], F32, name=f"spread_{e}", tag=f"turn_{e}")
-                for j in range(4):
-                    nc.tensor.transpose(
-                        spread[:, j, :], b_raw[:, 2 * j + e : 2 * j + e + 1].to_broadcast([P, P]), ident[:]
-                    )
+                spread = psum.tile([P, PACK, P], F32, name=f"spread_{e}", tag=f"turn_{e}")
+                for j in range(PACK):
+                    column = bias_rows[:, E * j + e : E * j + e + 1]
+                    nc.tensor.transpose(spread[:, j, :], column.to_broadcast([P, P]), identity[:])
                 for s in (2 * e, 2 * e + 1):
                     nc.scalar.activation(
-                        out=gated_bias[s][:].rearrange("s (q j) -> s q j", j=4),
+                        out=gated_bias[s][:].rearrange("s (q j) -> s q j", j=PACK),
                         in_=spread[:].rearrange("s j q -> s q j"),
                         func=COPY,
-                        scale=gate_col[:, s : s + 1],
+                        scale=gate_column[:, s : s + 1],
                     )
 
-        xb = [keep.tile([P, T, 4], BF16, name=f"xb_{a}", align_bytes=64) for a in range(PASSES)]
-        halves = (3, 4)
-        slot_words = {}
-        for a in range(PASSES):
-            for e in range(E):
-                if a in halves:
-                    slot_words[(a, e)] = keep.tile([P, C], U32, name=f"slot_words_{a}_{e}", align_bytes=64)[:]
-            if a not in halves:
-                whole = keep.tile([P, S], U32, name=f"slot_words_{a}", align_bytes=64)
-                slot_words[(a, None)] = whole[:]
-                for e in range(E):
-                    slot_words[(a, e)] = whole[:, e * C : (e + 1) * C]
-        pieces = {
-            0: [("vector", 0, 256), ("scalar", 256, 384)],
-            1: [("scalar", 0, 512), ("scalar", 512, 128)],
-            2: [("scalar", 0, 512), ("scalar", 512, 128)],
-            3: [("scalar", 0, 512), ("scalar", 512, 128)],
-            4: [("scalar", 0, 256), ("vector", 256, 256), ("vector", 512, 128)],
-        }
-        widths = {0: [(0, 256), (256, 256), (512, 128)], 1: [(0, 512), (512, 128)], 2: [(0, 512), (512, 128)], 3: [(0, 512), (512, 128)], 4: [(256, 256), (512, 128), (0, 256)]}
-
-        def casts(a, which):
-            for engine, t0, n in pieces[a]:
-                if engine == which:
-                    c0 = [u for u, m in chunks[a] if u <= t0][-1]
-                    cast(engine, xb[a][:, t0 : t0 + n, :], raw[(a, c0)][:, :, t0 - c0 : t0 - c0 + n])
-
-        def quantise(a):
-            for t0, n in widths[a]:
-                nc.vector.quantize_mx(
-                    out=words[a][:, t0 : t0 + n].bitcast(FP8X4),
-                    scales=plane[a][place[a] : P, t0 : t0 + n],
-                    in_=xb[a][:, t0 : t0 + n, :].rearrange("p t j -> p (t j)"),
-                )
-
-        def slots(e):
-            return (slice(0, S), offsets[:]) if e is None else (slice(e * C, (e + 1) * C), offsets[:, e * C // 16 : (e + 1) * C // 16])
-
-        def gather_words(a, e):
-            lists = slots(e)[1]
-            nc.vector.tensor_copy(slot_words[(a, e)], words[a][:].bitcast(U32).indirect(lists))
-
-        def gather_scales(g, e):
-            lists = slots(e)[1]
-            first = packs[g][0]
-            nc.vector.tensor_copy(slot_scales[(first, e)], plane[first][:].indirect(lists))
-            for a in packs[g][1:]:
-                k = place[a]
-                nc.sync.dma_start(
-                    out=slot_scales[(a, e)][0 : P - k, :].bitcast(I32), in_=slot_scales[(first, e)][k:P, :].bitcast(I32)
-                )
-
-        y = [psum.tile([P, N], F32, name=f"y_{s}") for s in range(TILES)]
-        order = (1, 2, 3, 0, 4)
-
-        def multiply(e, passes):
-            for a in passes:
-                for s in (2 * e, 2 * e + 1):
-                    cols = slice((s - 2 * e) * P, (s - 2 * e + 1) * P)
-                    nc.tensor.matmul_mx(
-                        out=y[s][:],
-                        lhsT=slot_words[(a, e)][:, cols].bitcast(FP8X4),
-                        lhsT_scale=slot_scales[(a, e)][:, cols],
-                        rhs=wq[e][:, a, :].bitcast(FP4X4),
-                        rhs_scale=ws[:, e * PASSES + a, :],
-                        start=(a == order[0]),
-                        stop=(a == order[-1]),
-                    )
-
-        wp_b = keep.tile([P, M, 4], BF16, name="wp_b", align_bytes=64)
+        wp_rounded = keep.tile([P, M, PACK], BF16, name="wp_rounded", align_bytes=64)
         wp_words = keep.tile([P, M], U32, name="wp_words", align_bytes=64)
         wp_scales = keep.tile([P, M], U8, name="wp_scales", align_bytes=64)
 
-        def project_weights():
-            cast("scalar", wp_b[:], wp_raw[:])
+        def quantise_wp():
+            round_and_interleave("scalar", wp_rounded[:], wp_raw[:])
             nc.vector.quantize_mx(
-                out=wp_words[:].bitcast(FP8X4), scales=wp_scales[:], in_=wp_b[:].rearrange("p f j -> p (f j)")
+                out=wp_words[:].bitcast(FP8X4), scales=wp_scales[:], in_=wp_rounded[:].rearrange("p f j -> p (f j)")
             )
 
+        c = [keep.tile([P, N], BF16, name=f"c_{s}", align_bytes=64) for s in range(TILES)]
+        c_turned = [keep.tile([P, P, PACK], BF16, name=f"c_turned_{s}", align_bytes=64) for s in range(TILES)]
         c_words = keep.tile([P, S], U32, name="c_words", align_bytes=64)
         c_scales = keep.tile([P, S], U8, name="c_scales", align_bytes=64)
-        c = [keep.tile([P, N], BF16, name=f"c_{s}", align_bytes=64) for s in range(TILES)]
-        cT = [keep.tile([P, P, 4], BF16, name=f"cT_{s}", align_bytes=64) for s in range(TILES)]
-        z_sb = [keep.tile([P, FT, P], F32, name=f"z_sb_{s}") for s in range(TILES)]
-        turned = {}
-        z = {}
+        z_copy = [keep.tile([P, FT, P], F32, name=f"z_copy_{s}") for s in range(TILES)]
+        turn_bank, z_bank = {}, {}
 
-        def evacuate(s):
+        def finish_tile(s):
             nc.vector.scalar_tensor_tensor(
-                out=c[s][:], in0=y[s][:], scalar=gate_col[:, s : s + 1], in1=gated_bias[s][:], op0=MULT, op1=ADD
+                out=c[s][:], in0=y[s][:], scalar=gate_column[:, s : s + 1], in1=gated_bias[s][:], op0=MULT, op1=ADD
             )
 
-        def turn(s):
+        def turn_tile(s):
             e, h = divmod(s, 2)
             if h == 0:
-                turned[e] = psum.tile([P, 2, 2, P], F32, name=f"turned_{e}", tag=f"turn_{e}")
+                turn_bank[e] = psum.tile([P, 2, 2, P], F32, name=f"turned_{e}", tag=f"turn_{e}")
             pairs = c[s][:].bitcast(F32)
             for u in range(2):
-                nc.tensor.transpose(turned[e][:, h, u, :], pairs[:, u : N // 2 : 2], ident[:])
+                nc.tensor.transpose(turn_bank[e][:, h, u, :], pairs[:, u : N // 2 : 2], identity[:])
             nc.scalar.copy(
-                out=cT[s][:].rearrange("p r j -> p (r j)").bitcast(F32).rearrange("p (r u) -> p r u", u=2),
-                in_=turned[e][:, h, :, :].rearrange("p u r -> p r u"),
+                out=c_turned[s][:].rearrange("p r j -> p (r j)").bitcast(F32).rearrange("p (r u) -> p r u", u=2),
+                in_=turn_bank[e][:, h, :, :].rearrange("p u r -> p r u"),
             )
 
-        def project(s):
+        def project_tile(s):
             e, h = divmod(s, 2)
-            cols = slice(s * P, (s + 1) * P)
+            slots = slice(s * P, (s + 1) * P)
             nc.vector.quantize_mx(
-                out=c_words[:, cols].bitcast(FP8X4), scales=c_scales[:, cols], in_=cT[s][:].rearrange("p r j -> p (r j)")
+                out=c_words[:, slots].bitcast(FP8X4),
+                scales=c_scales[:, slots],
+                in_=c_turned[s][:].rearrange("p r j -> p (r j)"),
             )
             if h == 0:
-                z[e] = psum.tile([P, 2, FT, P], F32, name=f"z_{e}")
+                z_bank[e] = psum.tile([P, 2, FT, P], F32, name=f"z_{e}")
             for f in range(FT):
-                fcols = slice(f * P, (f + 1) * P)
+                outputs = slice(f * P, (f + 1) * P)
                 nc.tensor.matmul_mx(
-                    out=z[e][:, h, f, :],
-                    lhsT=wp_words[:, fcols].bitcast(FP8X4),
-                    lhsT_scale=wp_scales[:, fcols],
-                    rhs=c_words[:, cols].bitcast(FP8X4),
-                    rhs_scale=c_scales[:, cols],
+                    out=z_bank[e][:, h, f, :],
+                    lhsT=wp_words[:, outputs].bitcast(FP8X4),
+                    lhsT_scale=wp_scales[:, outputs],
+                    rhs=c_words[:, slots].bitcast(FP8X4),
+                    rhs_scale=c_scales[:, slots],
                     start=True,
                     stop=True,
                 )
-            nc.scalar.activation(out=z_sb[s][:], in_=z[e][:, h, :, :], func=COPY)
+            nc.scalar.activation(out=z_copy[s][:], in_=z_bank[e][:, h, :, :], func=COPY)
 
-        def scatter(s):
+        def scatter_tile(s):
+            places = offsets[:, s * P // LIST : (s + 1) * P // LIST]
             for f in range(FT):
-                nc.vector.tensor_copy(placed[f][:].indirect(offsets[:, s * P // 16 : (s + 1) * P // 16]), z_sb[s][:, f, :])
+                nc.vector.tensor_copy(out_tile[f][:].indirect(places), z_copy[s][:, f, :])
 
-        casts(0, "scalar")
-        casts(0, "vector")
-        quantise(0)
-        casts(1, "scalar")
-        casts(1, "vector")
-        gather_words(0, None)
-        quantise(1)
-        gather_scales(0, None)
-        gather_words(1, None)
-        casts(2, "scalar")
-        casts(2, "vector")
-        quantise(2)
-        casts(3, "scalar")
-        casts(3, "vector")
-        gather_words(2, None)
-        gather_scales(1, None)
-        quantise(3)
-        casts(4, "scalar")
-        casts(4, "vector")
+        round_tokens(0)
+        quantise_tokens(0)
+        round_tokens(1)
+        gather_words(0, "all")
+        quantise_tokens(1)
+        gather_scales(1, "all")
+        nc.sync.dma_start(
+            out=slot_scales[(0, "all")][0 : P - SHARED_ROW, :].bitcast(I32),
+            in_=slot_scales[(1, "all")][SHARED_ROW:P, :].bitcast(I32),
+        )
+        gather_words(1, "all")
+        round_tokens(2)
+        quantise_tokens(2)
+        round_tokens(3)
+        gather_words(2, "all")
+        gather_scales(2, "all")
+        quantise_tokens(3)
+        round_tokens(4)
         spread_bias()
         gather_words(3, 0)
-        gather_scales(2, 0)
-        quantise(4)
-        gather_words(4, 0)
         gather_scales(3, 0)
-        gather_words(3, 1)
-        gather_scales(2, 1)
-        gather_words(4, 1)
-        gather_scales(3, 1)
-        multiply(0, order)
-        project_weights()
-        multiply(1, order)
+        quantise_tokens(4)
+        gather_words(4, 0)
+        gather_scales(4, 0)
+        for a in SPLIT_PASSES:
+            gather_words(a, 1)
+            gather_scales(a, 1)
+        multiply(0)
+        quantise_wp()
+        multiply(1)
+
         for s in range(TILES):
-            evacuate(s)
-            turn(s)
+            finish_tile(s)
+            turn_tile(s)
         for s in range(TILES):
-            project(s)
+            project_tile(s)
         for s in range(TILES):
-            scatter(s)
+            scatter_tile(s)
         for f in range(FT):
-            nc.sync.dma_start(out=out[f * P : (f + 1) * P, :], in_=placed[f][:])
+            nc.sync.dma_start(out=out[f * P : (f + 1) * P, :], in_=out_tile[f][:])

from contextlib import ExitStack

import concourse.mybir as mybir
from concourse.masks import make_identity

K, T, E, C, N, M = 2560, 640, 2, 256, 512, 256
P = 128
PACK = 4
PASSES = K // (P * PACK)
S = E * C
TILES = S // P
FT = M // P
LIST = 16

WORD_COLUMNS = 688
BYTE_COLUMNS = 704

SHARED_ROW = 4

LOADS = (((0, 256), (256, 384)), ((0, 640),), ((0, 640),), ((0, 640),), ((0, 512), (512, 128)))
CASTS = (
    (("vector", 0, 256), ("vector", 256, 384)),
    (("scalar", 256, 256), ("vector", 0, 256), ("vector", 512, 128)),
    (("scalar", 0, 512), ("vector", 512, 128)),
    (("scalar", 0, 512), ("scalar", 512, 128)),
    (("scalar", 0, 256), ("scalar", 256, 256), ("scalar", 512, 128)),
)
QUANTISED = (
    ((0, 256), (256, 256), (512, 128)),
    ((0, 256), (512, 128), (256, 256)),
    ((512, 128), (0, 512)),
    ((0, 512), (512, 128)),
    ((0, 256), (256, 256), (512, 128)),
)
WHOLE_PASSES = (0, 1, 2)
SPLIT_PASSES = (3, 4)
ORDER = (1, 2, 3, 0, 4)

FLOPS = 2 * K * N * S + 2 * N * M * T
BYTES = 4 * (K * T + N * E + N * M + S + M * T) + E * PASSES * (2 * P * N + 16 * N) + 2 * P * S // LIST

F32 = mybir.dt.float32
BF16 = mybir.dt.bfloat16
I32 = mybir.dt.int32
U32 = mybir.dt.uint32
U16 = mybir.dt.uint16
U8 = mybir.dt.uint8
FP8X4 = mybir.dt.float8_e4m3fn_x4
FP4X4 = mybir.dt.float4_e2m1fn_x4
COPY = mybir.ActivationFunctionType.Copy
MULT = mybir.AluOpType.mult
ADD = mybir.AluOpType.add


def tile_moe_nxt_lin_bias_kernel(tc, xT, w_words, w_scales, b, wp, gate, offs, out):
    nc = tc.nc

    def round_and_interleave(engine, dst, src):
        dst = dst.rearrange("p (c i) j -> p c j i", i=4)
        src = src.rearrange("p j (c i) -> p c j i", i=4)
        if engine == "scalar":
            nc.scalar.activation(out=dst, in_=src, func=COPY)
        else:
            nc.vector.tensor_copy(dst, src)

    with ExitStack() as ctx:
        keep = ctx.enter_context(tc.tile_pool(name="keep", bufs=1))
        psum = ctx.enter_context(tc.psum_pool(name="psum", bufs=1))

        early = keep.tile([P, 1], F32, name="early")
        nc.gpsimd.memset(early[:], 0.0)
        early_copy = keep.tile([P, 1], F32, name="early_copy")
        nc.scalar.activation(out=early_copy[:], in_=early[:], func=COPY)

        offsets = keep.tile([P, S // LIST], U16, name="offsets")
        bias_rows = keep.tile([P, PACK * E], F32, name="bias_rows")
        gate_column = keep.tile([P, TILES], F32, name="gate_column")
        w_bytes = keep.tile([P, E * PASSES, N], U8, name="w_bytes", align_bytes=64)
        w_codes = [keep.tile([P, PASSES, 2 * N], U8, name=f"w_codes_{e}", align_bytes=64) for e in range(E)]
        wp_raw = keep.tile([P, PACK, M], F32, name="wp_raw")
        x_raw = {}

        nc.vector.memset(w_bytes[:].rearrange("p g n -> p (g n)").bitcast(I32), 0)

        for a in range(PASSES):
            rows = xT[P * PACK * a : P * PACK * (a + 1), :].rearrange("(p j) t -> p j t", j=PACK)
            for t0, n in LOADS[a]:
                piece = keep.tile([P, PACK, n], F32, name=f"x_raw_{a}_{t0}")
                nc.sync.dma_start(out=piece[:], in_=rows[:, :, t0 : t0 + n])
                x_raw[(a, t0)] = piece
                if (a, t0) == (0, 0):
                    nc.sync.dma_start(offsets[:], offs)
            if a == 1:
                nc.sync.dma_start(out=bias_rows[:], in_=b.rearrange("(p j) e -> p (j e)", j=PACK))
                diagonal = gate.rearrange("n s -> (n s)")[0 : P * (S + 1)].rearrange("(p r) -> p r", r=S + 1)
                with nc.allow_non_contiguous_dma(reason="one gate a partition"):
                    nc.sync.dma_start(out=gate_column[:], in_=diagonal[:, 0:S:P])

        byte_rows = w_scales.rearrange("e a (q r) n -> r q (e a) n", r=4)
        for r in range(4):
            nc.sync.dma_start(out=w_bytes[r:P:32, :, :].bitcast(I32), in_=byte_rows[r].bitcast(I32))

        def load_expert(e):
            nc.sync.dma_start(out=w_codes[e][:].bitcast(I32), in_=w_words[e].rearrange("a p c -> p a c").bitcast(I32))

        load_expert(0)
        nc.sync.dma_start(out=wp_raw[:], in_=wp.rearrange("(p j) f -> p j f", j=PACK))
        load_expert(1)

        identity = keep.tile([P, P], F32, name="identity")
        make_identity(nc, identity[:])

        words = [keep.tile([P, WORD_COLUMNS], I32, name=f"words_{a}", align_bytes=64) for a in range(PASSES)]
        for a in range(PASSES):
            nc.vector.memset(words[a][:, T:WORD_COLUMNS], 0)
        scales = {}
        for a in range(1, PASSES):
            scales[a] = keep.tile([P, BYTE_COLUMNS], U8, name=f"scales_{a}", align_bytes=64)
            nc.gpsimd.memset(scales[a][:, T:BYTE_COLUMNS], 0)
        scales[0] = scales[1]

        slot_words, slot_scales = {}, {}
        for a in WHOLE_PASSES:
            words_tile = keep.tile([P, S], U32, name=f"slot_words_{a}", align_bytes=64)
            bytes_tile = keep.tile([P, S], U8, name=f"slot_scales_{a}", align_bytes=64)
            slot_words[(a, "all")], slot_scales[(a, "all")] = words_tile[:], bytes_tile[:]
            for e in range(E):
                slot_words[(a, e)] = words_tile[:, e * C : (e + 1) * C]
                slot_scales[(a, e)] = bytes_tile[:, e * C : (e + 1) * C]
        for a in SPLIT_PASSES:
            for e in range(E):
                words_tile = keep.tile([P, C], U32, name=f"slot_words_{a}_{e}", align_bytes=64)
                bytes_tile = keep.tile([P, C], U8, name=f"slot_scales_{a}_{e}", align_bytes=64)
                slot_words[(a, e)], slot_scales[(a, e)] = words_tile[:], bytes_tile[:]
        nc.gpsimd.memset(slot_scales[(0, "all")].bitcast(I32), 0)

        out_tile = [keep.tile([P, T], F32, name=f"out_tile_{f}") for f in range(FT)]
        for f in range(FT):
            nc.gpsimd.memset(out_tile[f][:], 0.0)

        x_rounded = [keep.tile([P, T, PACK], BF16, name=f"x_rounded_{a}", align_bytes=64) for a in range(PASSES)]

        def round_tokens(a):
            for engine, t0, n in CASTS[a]:
                start = max(u for u, count in LOADS[a] if u <= t0)
                round_and_interleave(
                    engine, x_rounded[a][:, t0 : t0 + n, :], x_raw[(a, start)][:, :, t0 - start : t0 - start + n]
                )

        def quantise_tokens(a):
            row = SHARED_ROW if a == 0 else 0
            for t0, n in QUANTISED[a]:
                nc.vector.quantize_mx(
                    out=words[a][:, t0 : t0 + n].bitcast(FP8X4),
                    scales=scales[a][row:P, t0 : t0 + n],
                    in_=x_rounded[a][:, t0 : t0 + n, :].rearrange("p t j -> p (t j)"),
                )

        def slot_list(e):
            return offsets[:] if e == "all" else offsets[:, e * C // LIST : (e + 1) * C // LIST]

        def gather_words(a, e):
            nc.vector.tensor_copy(slot_words[(a, e)], words[a][:].bitcast(U32).indirect(slot_list(e)))

        def gather_scales(a, e):
            nc.vector.tensor_copy(slot_scales[(a, e)], scales[a][:].indirect(slot_list(e)))

        y = [psum.tile([P, N], F32, name=f"y_{s}") for s in range(TILES)]

        def multiply(e):
            for a in ORDER:
                for h in range(2):
                    slots = slice(h * P, (h + 1) * P)
                    nc.tensor.matmul_mx(
                        out=y[2 * e + h][:],
                        lhsT=slot_words[(a, e)][:, slots].bitcast(FP8X4),
                        lhsT_scale=slot_scales[(a, e)][:, slots],
                        rhs=w_codes[e][:, a, :].bitcast(FP4X4),
                        rhs_scale=w_bytes[:, e * PASSES + a, :],
                        start=(a == ORDER[0]),
                        stop=(a == ORDER[-1]),
                    )

        gated_bias = [keep.tile([P, N], F32, name=f"gated_bias_{s}") for s in range(TILES)]

        def spread_bias():
            for e in range(E):
                spread = psum.tile([P, PACK, P], F32, name=f"spread_{e}", tag=f"turn_{e}")
                for j in range(PACK):
                    column = bias_rows[:, E * j + e : E * j + e + 1]
                    nc.tensor.transpose(spread[:, j, :], column.to_broadcast([P, P]), identity[:])
                for s in (2 * e, 2 * e + 1):
                    nc.scalar.activation(
                        out=gated_bias[s][:].rearrange("s (q j) -> s q j", j=PACK),
                        in_=spread[:].rearrange("s j q -> s q j"),
                        func=COPY,
                        scale=gate_column[:, s : s + 1],
                    )

        wp_rounded = keep.tile([P, M, PACK], BF16, name="wp_rounded", align_bytes=64)
        wp_words = keep.tile([P, M], U32, name="wp_words", align_bytes=64)
        wp_scales = keep.tile([P, M], U8, name="wp_scales", align_bytes=64)

        def quantise_wp():
            round_and_interleave("scalar", wp_rounded[:], wp_raw[:])
            nc.vector.quantize_mx(
                out=wp_words[:].bitcast(FP8X4), scales=wp_scales[:], in_=wp_rounded[:].rearrange("p f j -> p (f j)")
            )

        c = [keep.tile([P, N], BF16, name=f"c_{s}", align_bytes=64) for s in range(TILES)]
        c_turned = [keep.tile([P, P, PACK], BF16, name=f"c_turned_{s}", align_bytes=64) for s in range(TILES)]
        c_words = keep.tile([P, S], U32, name="c_words", align_bytes=64)
        c_scales = keep.tile([P, S], U8, name="c_scales", align_bytes=64)
        z_copy = [keep.tile([P, FT, P], F32, name=f"z_copy_{s}") for s in range(TILES)]
        turn_bank, z_bank = {}, {}

        def finish_tile(s):
            nc.vector.scalar_tensor_tensor(
                out=c[s][:], in0=y[s][:], scalar=gate_column[:, s : s + 1], in1=gated_bias[s][:], op0=MULT, op1=ADD
            )

        def turn_tile(s):
            e, h = divmod(s, 2)
            if h == 0:
                turn_bank[e] = psum.tile([P, 2, 2, P], F32, name=f"turned_{e}", tag=f"turn_{e}")
            pairs = c[s][:].bitcast(F32)
            for u in range(2):
                nc.tensor.transpose(turn_bank[e][:, h, u, :], pairs[:, u : N // 2 : 2], identity[:])
            nc.scalar.copy(
                out=c_turned[s][:].rearrange("p r j -> p (r j)").bitcast(F32).rearrange("p (r u) -> p r u", u=2),
                in_=turn_bank[e][:, h, :, :].rearrange("p u r -> p r u"),
            )

        def project_tile(s):
            e, h = divmod(s, 2)
            slots = slice(s * P, (s + 1) * P)
            nc.vector.quantize_mx(
                out=c_words[:, slots].bitcast(FP8X4),
                scales=c_scales[:, slots],
                in_=c_turned[s][:].rearrange("p r j -> p (r j)"),
            )
            if h == 0:
                z_bank[e] = psum.tile([P, 2, FT, P], F32, name=f"z_{e}")
            for f in range(FT):
                outputs = slice(f * P, (f + 1) * P)
                nc.tensor.matmul_mx(
                    out=z_bank[e][:, h, f, :],
                    lhsT=wp_words[:, outputs].bitcast(FP8X4),
                    lhsT_scale=wp_scales[:, outputs],
                    rhs=c_words[:, slots].bitcast(FP8X4),
                    rhs_scale=c_scales[:, slots],
                    start=True,
                    stop=True,
                )
            nc.scalar.activation(out=z_copy[s][:], in_=z_bank[e][:, h, :, :], func=COPY)

        def scatter_tile(s):
            places = offsets[:, s * P // LIST : (s + 1) * P // LIST]
            for f in range(FT):
                nc.vector.tensor_copy(out_tile[f][:].indirect(places), z_copy[s][:, f, :])

        round_tokens(0)
        quantise_tokens(0)
        round_tokens(1)
        gather_words(0, "all")
        quantise_tokens(1)
        gather_scales(1, "all")
        nc.sync.dma_start(
            out=slot_scales[(0, "all")][0 : P - SHARED_ROW, :].bitcast(I32),
            in_=slot_scales[(1, "all")][SHARED_ROW:P, :].bitcast(I32),
        )
        gather_words(1, "all")
        round_tokens(2)
        quantise_tokens(2)
        round_tokens(3)
        gather_words(2, "all")
        gather_scales(2, "all")
        quantise_tokens(3)
        round_tokens(4)
        spread_bias()
        gather_words(3, 0)
        gather_scales(3, 0)
        quantise_tokens(4)
        gather_words(4, 0)
        gather_scales(4, 0)
        for a in SPLIT_PASSES:
            gather_words(a, 1)
            gather_scales(a, 1)
        multiply(0)
        quantise_wp()
        multiply(1)

        for s in range(TILES):
            finish_tile(s)
            turn_tile(s)
        for s in range(TILES):
            project_tile(s)
        for s in range(TILES):
            scatter_tile(s)
        for f in range(FT):
            nc.sync.dma_start(out=out[f * P : (f + 1) * P, :], in_=out_tile[f][:])
